import numpy as np
import ml_dtypes


def mxq(x, axis, fmt="e4m3"):
    dtype, down = {"e4m3": (ml_dtypes.float8_e4m3fn, 7), "e5m2": (ml_dtypes.float8_e5m2, 14)}[fmt]
    v = np.moveaxis(np.asarray(x, np.float32).astype(ml_dtypes.bfloat16).astype(np.float64), axis, -1)
    blocks = v.reshape(v.shape[:-1] + (-1, 32))
    amax = np.abs(blocks).max(-1, keepdims=True)
    byte = np.maximum(np.where(amax > 0, np.frexp(amax)[1] - 1 + 127, 0) - down, 1)
    scale = np.exp2(byte - 127.0)
    codes = (blocks / scale).astype(np.float32).astype(dtype).astype(np.float64)
    return np.moveaxis((codes * scale).reshape(v.shape), -1, axis)


WIDE = False


def mx_kscale(k, group=512):
    if not WIDE:
        return np.ones(k)
    levels = np.array([18, -18])
    if group != 512:
        return np.exp2(np.random.permutation(np.resize(levels, k // group))).repeat(group)
    if k % 512:
        return np.exp2(np.random.permutation(np.resize(levels, k // 32))).repeat(32)
    a = np.empty((k // 512, 16))
    for p in range(k // 512):
        a[p, :8] = np.random.permutation(np.resize(levels, 8))
        for g in range(8):
            far = levels[np.abs(levels - a[p, g]) >= 10]
            a[p, g + 8] = far[np.random.randint(len(far))]
    return np.exp2(a.ravel()).repeat(32)


def f64(x):
    return np.asarray(x).astype(np.float64)


def sigmoid(v):
    return 1.0 / (1.0 + np.exp(-v))


def bf(x):
    return np.asarray(x, np.float32).astype(ml_dtypes.bfloat16)


def planes(Y):
    r, m = Y.shape
    b = f64(bf(Y)).reshape(r // 32, 32, m)
    amax = np.abs(b).max(1)
    byte = np.clip(np.where(amax > 0, np.frexp(amax)[1] - 1 + 127 - 7, 1), 1, 254)
    codes = (b * np.exp2(127.0 - byte)[:, None, :]).reshape(r, m).astype(np.float32).astype(ml_dtypes.float8_e4m3fn).view(np.uint8)
    words = codes.reshape(r // 512, 128, 4, m).transpose(0, 1, 3, 2)
    return np.ascontiguousarray(words), np.ascontiguousarray(byte.astype(np.uint8).reshape(r // 512, 16, m))


G, D, M, N, L = 4, 128, 128, 512, 640


def setup_inputs():
    n = np.random.standard_normal
    s_d = mx_kscale(D, 0)
    return {
        "x": (n((G, D, L)) * s_d[:, None]).astype(np.float32),
        "w0": (n((G, D, M)) / np.sqrt(2 * D) / s_d[:, None]).astype(np.float32),
        "w1": (n((G, D, M)) / np.sqrt(2 * D) / s_d[:, None]).astype(np.float32),
        "u0": (n((G, D, M)) / np.sqrt(2 * D) / s_d[:, None]).astype(np.float32),
        "u1": (n((G, D, M)) / np.sqrt(2 * D) / s_d[:, None]).astype(np.float32),
    }


def reference(x, w0, w1, u0, u1):
    w0q = mxq(f64(w0), 1, "e4m3")
    xq = mxq(f64(x), 1, "e4m3")
    w1q = mxq(f64(w1), 1, "e4m3")
    z = (w0q.transpose(0, 2, 1) @ xq[..., :512]) + (w1q.transpose(0, 2, 1) @ xq[..., 128 : 640])
    u0q = mxq(f64(u0), 1, "e4m3")
    u1q = mxq(f64(u1), 1, "e4m3")
    g_ = (u0q.transpose(0, 2, 1) @ xq[..., :512]) + (u1q.transpose(0, 2, 1) @ xq[..., 128 : 640])
    y = np.tanh(z) * sigmoid(g_)
    Y = y.reshape(G * M, N)
    words, scales = planes(Y)
    return Y, words, scales

@@ -1,0 +1,181 @@
+from contextlib import ExitStack
+
+import concourse.mybir as mybir
+
+G, D, M, N, DILATION = 4, 128, 128, 512, 128
+L = N + DILATION
+FLOPS = 2 * 4 * G * D * M * N
+
+F32 = mybir.dt.float32
+BF16 = mybir.dt.bfloat16
+I32 = mybir.dt.int32
+U32 = mybir.dt.uint32
+U8 = mybir.dt.uint8
+FP8X4 = mybir.dt.float8_e4m3fn_x4
+ACT = mybir.ActivationFunctionType
+ALU = mybir.AluOpType
+
+P = 128
+PACK = 4
+ROWS = D // PACK
+RUN = 4
+X_PARTS = [(0, 256), (256, 128), (384, 256)]
+PIECES = [(0, 256), (256, 256)]
+
+
+def interleave(copy, packed, raw):
+    copy(
+        out=packed.rearrange("p (c i) j -> p c j i", i=RUN),
+        in_=raw.rearrange("p j (c i) -> p c j i", i=RUN),
+    )
+
+
+def quantize(nc, codes, scales, packed):
+    nc.vector.quantize_mx(
+        out=codes.bitcast(FP8X4), scales=scales, in_=packed.rearrange("p c j -> p (c j)")
+    )
+
+
+def tile_rows_pl_conv_wave_kernel(tc, x, w0, w1, u0, u1, out_0, out_1, out_2):
+    nc = tc.nc
+    weights = [w0, w1, u0, u1]
+    with ExitStack() as ctx:
+        sb = ctx.enter_context(tc.tile_pool(name="sb", bufs=1))
+        ps = ctx.enter_context(tc.psum_pool(name="ps", bufs=1))
+        ctx.enter_context(tc.manual_schedule())
+
+        x_raw = sb.tile([P, PACK, L], F32, name="x_raw", align_bytes=64)
+        nc.sync.dma_start(out=x_raw[:], in_=x.rearrange("g (p j) l -> (g p) j l", j=PACK))
+        w_raw = []
+        for k, w in enumerate(weights):
+            t = sb.tile([P, PACK, M], F32, name="w_raw%d" % k, align_bytes=64)
+            nc.sync.dma_start(out=t[:], in_=w.rearrange("g (p j) m -> (g p) j m", j=PACK))
+            w_raw.append(t)
+
+        warm_in = sb.tile([P, 8], F32, name="warm_in")
+        warm_out = sb.tile([P, 8], F32, name="warm_out")
+        nc.vector.memset(warm_in[:], 0.0)
+        nc.scalar.activation(out=warm_out[:], in_=warm_in[:], func=ACT.Sigmoid)
+
+        x_packed = [
+            sb.tile([P, width, PACK], BF16, name="x_packed%d" % k, align_bytes=64)
+            for k, (start, width) in enumerate(X_PARTS)
+        ]
+        x_codes = sb.tile([P, L], U32, name="x_codes", align_bytes=64)
+        x_scales = sb.tile([P, L], U8, name="x_scales", align_bytes=64)
+        w_packed = [sb.tile([P, M, PACK], BF16, name="w_packed%d" % k, align_bytes=64) for k in range(4)]
+        w_codes = [sb.tile([P, M], U32, name="w_codes%d" % k, align_bytes=64) for k in range(4)]
+        w_scales = [sb.tile([P, M], U8, name="w_scales%d" % k, align_bytes=64) for k in range(4)]
+
+        def pack_x(copy, k):
+            start, width = X_PARTS[k]
+            interleave(copy, x_packed[k][:], x_raw[:, :, start : start + width])
+
+        def quantize_x(k):
+            start, width = X_PARTS[k]
+            cols = slice(start, start + width)
+            quantize(nc, x_codes[:, cols], x_scales[:, cols], x_packed[k][:])
+
+        def pack_w(copy, k):
+            interleave(copy, w_packed[k][:], w_raw[k][:])
+
+        def quantize_w(k):
+            quantize(nc, w_codes[k][:], w_scales[k][:], w_packed[k][:])
+
+        z_sum = [ps.tile([P, N], F32, name="z_sum%d" % g) for g in range(G)]
+        gate_sum = [ps.tile([P, N], F32, name="gate_sum%d" % g) for g in range(G)]
+
+        def tap(sums, k):
+            t = k % 2
+            cols = slice(t * DILATION, t * DILATION + N)
+            for g in range(G):
+                rows = slice(ROWS * g, ROWS * (g + 1))
+                nc.tensor.matmul_mx(
+                    out=sums[g][:],
+                    lhsT=w_codes[k][rows, :].bitcast(FP8X4),
+                    lhsT_scale=w_scales[k][rows, :],
+                    rhs=x_codes[rows, cols].bitcast(FP8X4),
+                    rhs_scale=x_scales[rows, cols],
+                    start=(t == 0),
+                    stop=(t == 1),
+                )
+
+        pack_x(nc.scalar.copy, 2)
+        pack_w(nc.scalar.copy, 0)
+        pack_x(nc.vector.tensor_copy, 0)
+        pack_x(nc.vector.tensor_copy, 1)
+        quantize_x(0)
+        quantize_x(1)
+        pack_w(nc.vector.tensor_copy, 1)
+        quantize_x(2)
+        quantize_w(0)
+        tap(z_sum, 0)
+        quantize_w(1)
+        tap(z_sum, 1)
+        pack_w(nc.vector.tensor_copy, 2)
+        pack_w(nc.vector.tensor_copy, 3)
+        quantize_w(2)
+        tap(gate_sum, 2)
+        quantize_w(3)
+        tap(gate_sum, 3)
+
+        tanh_z, gate, y, y_round, y_rows, y_packed, y_codes = [], [], [], [], [], [], []
+        for h, (start, width) in enumerate(PIECES):
+            tanh_z.append([sb.tile([P, width], F32, name="tanh%d_%d" % (h, g)) for g in range(G)])
+            gate.append([sb.tile([P, width], F32, name="gate%d_%d" % (h, g)) for g in range(G)])
+            y.append(sb.tile([P, G, width], F32, name="y%d" % h))
+            y_round.append([sb.tile([P, width], BF16, name="y_round%d_%d" % (h, g)) for g in range(G)])
+            y_rows.append(sb.tile([P, PACK, width], BF16, name="y_rows%d" % h, align_bytes=64))
+            y_packed.append(sb.tile([P, width, PACK], BF16, name="y_packed%d" % h, align_bytes=64))
+            y_codes.append(sb.tile([P, width], U32, name="y_codes%d" % h, align_bytes=64))
+        y_scales = sb.tile([P, N], U8, name="y_scales", align_bytes=64)
+
+        def columns(h):
+            start, width = PIECES[h]
+            return slice(start, start + width)
+
+        def do_tanh(h, g):
+            nc.scalar.activation(out=tanh_z[h][g][:], in_=z_sum[g][:, columns(h)], func=ACT.Tanh)
+
+        def do_gate(h, g):
+            nc.scalar.activation(out=gate[h][g][:], in_=gate_sum[g][:, columns(h)], func=ACT.Sigmoid)
+
+        for g in range(G):
+            do_tanh(0, g)
+        for g in range(G):
+            do_gate(0, g)
+        for h in range(1, len(PIECES)):
+            for g in range(G):
+                do_tanh(h, g)
+                do_gate(h, g)
+
+        y_out = out_0.rearrange("(g m) n -> m g n", g=G)
+        words_out = out_1[0].rearrange("p n u -> p (n u)").bitcast(I32)
+        scales_out = out_2[0].bitcast(I32)
+
+        def product(h, g):
+            nc.vector.tensor_tensor(out=y[h][:, g, :], in0=tanh_z[h][g][:], in1=gate[h][g][:], op=ALU.mult)
+
+        def round_and_regroup(h, g):
+            nc.vector.tensor_copy(out=y_round[h][g][:], in_=y[h][:, g, :])
+            nc.sync.dma_start(out=y_rows[h][ROWS * g : ROWS * (g + 1), :, :], in_=y_round[h][g][:])
+            if g == G - 1:
+                nc.sync.dma_start(out=y_out[:, :, columns(h)], in_=y[h][:])
+
+        units = [(h, g) for h in range(len(PIECES)) for g in range(G)]
+        for i, (h, g) in enumerate(units):
+            product(h, g)
+            if i > 0:
+                round_and_regroup(*units[i - 1])
+        round_and_regroup(*units[-1])
+
+        for h in range(len(PIECES)):
+            interleave(nc.vector.tensor_copy, y_packed[h][:], y_rows[h][:])
+            quantize(nc, y_codes[h][:], y_scales[:, columns(h)], y_packed[h][:])
+            nc.sync.dma_start(out=words_out[:, columns(h)], in_=y_codes[h][:].bitcast(I32))
+        for q in range(4):
+            queue = nc.sync if q < 2 else nc.scalar
+            queue.dma_start(
+                out=scales_out[4 * q : 4 * q + 4, :],
+                in_=y_scales[32 * q : 32 * q + 4, :].bitcast(I32),
+            )

@@ -19,7 +19,9 @@ P = 128
 PACK = 4
 ROWS = D // PACK
 RUN = 4
-X_PARTS = [(0, 256), (256, 128), (384, 256)]
+STEP = 128
+X_LOADS = [(0, 384), (384, 256)]
+ORDER = [0, 2, 1, 3]
 PIECES = [(0, 256), (256, 256)]
 
 
@@ -44,13 +46,26 @@ def tile_rows_pl_conv_wave_kernel(tc, x, w0, w1, u0, u1, out_0, out_1, out_2):
         ps = ctx.enter_context(tc.psum_pool(name="ps", bufs=1))
         ctx.enter_context(tc.manual_schedule())
 
-        x_raw = sb.tile([P, PACK, L], F32, name="x_raw", align_bytes=64)
-        nc.sync.dma_start(out=x_raw[:], in_=x.rearrange("g (p j) l -> (g p) j l", j=PACK))
-        w_raw = []
-        for k, w in enumerate(weights):
-            t = sb.tile([P, PACK, M], F32, name="w_raw%d" % k, align_bytes=64)
-            nc.sync.dma_start(out=t[:], in_=w.rearrange("g (p j) m -> (g p) j m", j=PACK))
-            w_raw.append(t)
+        x_rows = x.rearrange("g (p j) l -> (g p) j l", j=PACK)
+        x_raw = [
+            sb.tile([P, PACK, width], F32, name="x_raw%d" % k, align_bytes=64)
+            for k, (start, width) in enumerate(X_LOADS)
+        ]
+        w_raw = [sb.tile([P, PACK, M], F32, name="w_raw%d" % k, align_bytes=64) for k in range(4)]
+
+        def load_x(k):
+            start, width = X_LOADS[k]
+            nc.sync.dma_start(out=x_raw[k][:], in_=x_rows[:, :, start : start + width])
+
+        def load_w(k):
+            nc.sync.dma_start(out=w_raw[k][:], in_=weights[k].rearrange("g (p j) m -> (g p) j m", j=PACK))
+
+        load_w(0)
+        load_w(1)
+        load_x(0)
+        load_w(2)
+        load_w(3)
+        load_x(1)
 
         warm_in = sb.tile([P, 8], F32, name="warm_in")
         warm_out = sb.tile([P, 8], F32, name="warm_out")
@@ -58,23 +73,22 @@ def tile_rows_pl_conv_wave_kernel(tc, x, w0, w1, u0, u1, out_0, out_1, out_2):
         nc.scalar.activation(out=warm_out[:], in_=warm_in[:], func=ACT.Sigmoid)
 
         x_packed = [
-            sb.tile([P, width, PACK], BF16, name="x_packed%d" % k, align_bytes=64)
-            for k, (start, width) in enumerate(X_PARTS)
+            sb.tile([P, STEP, PACK], BF16, name="x_packed%d" % k, align_bytes=64)
+            for k in range(L // STEP)
         ]
-        x_codes = sb.tile([P, L], U32, name="x_codes", align_bytes=64)
-        x_scales = sb.tile([P, L], U8, name="x_scales", align_bytes=64)
+        x_codes = [sb.tile([P, STEP], U32, name="x_codes%d" % k, align_bytes=64) for k in range(L // STEP)]
+        x_scales = [sb.tile([P, STEP], U8, name="x_scales%d" % k, align_bytes=64) for k in range(L // STEP)]
         w_packed = [sb.tile([P, M, PACK], BF16, name="w_packed%d" % k, align_bytes=64) for k in range(4)]
         w_codes = [sb.tile([P, M], U32, name="w_codes%d" % k, align_bytes=64) for k in range(4)]
         w_scales = [sb.tile([P, M], U8, name="w_scales%d" % k, align_bytes=64) for k in range(4)]
 
         def pack_x(copy, k):
-            start, width = X_PARTS[k]
-            interleave(copy, x_packed[k][:], x_raw[:, :, start : start + width])
+            load = 0 if k * STEP < X_LOADS[1][0] else 1
+            first = k * STEP - X_LOADS[load][0]
+            interleave(copy, x_packed[k][:], x_raw[load][:, :, first : first + STEP])
 
         def quantize_x(k):
-            start, width = X_PARTS[k]
-            cols = slice(start, start + width)
-            quantize(nc, x_codes[:, cols], x_scales[:, cols], x_packed[k][:])
+            quantize(nc, x_codes[k][:], x_scales[k][:], x_packed[k][:])
 
         def pack_w(copy, k):
             interleave(copy, w_packed[k][:], w_raw[k][:])
@@ -85,49 +99,31 @@ def tile_rows_pl_conv_wave_kernel(tc, x, w0, w1, u0, u1, out_0, out_1, out_2):
         z_sum = [ps.tile([P, N], F32, name="z_sum%d" % g) for g in range(G)]
         gate_sum = [ps.tile([P, N], F32, name="gate_sum%d" % g) for g in range(G)]
 
-        def tap(sums, k):
-            t = k % 2
-            cols = slice(t * DILATION, t * DILATION + N)
-            for g in range(G):
-                rows = slice(ROWS * g, ROWS * (g + 1))
-                nc.tensor.matmul_mx(
-                    out=sums[g][:],
-                    lhsT=w_codes[k][rows, :].bitcast(FP8X4),
-                    lhsT_scale=w_scales[k][rows, :],
-                    rhs=x_codes[rows, cols].bitcast(FP8X4),
-                    rhs_scale=x_scales[rows, cols],
-                    start=(t == 0),
-                    stop=(t == 1),
-                )
+        def convolve(sums, first_weight, step, groups=ORDER):
+            cols = slice(step * STEP, (step + 1) * STEP)
+            for t in range(2):
+                k = first_weight + t
+                for g in groups:
+                    rows = slice(ROWS * g, ROWS * (g + 1))
+                    nc.tensor.matmul_mx(
+                        out=sums[g][:, cols],
+                        lhsT=w_codes[k][rows, :].bitcast(FP8X4),
+                        lhsT_scale=w_scales[k][rows, :],
+                        rhs=x_codes[step + t][rows, :].bitcast(FP8X4),
+                        rhs_scale=x_scales[step + t][rows, :],
+                        start=(t == 0),
+                        stop=(t == 1),
+                    )
 
-        pack_x(nc.scalar.copy, 2)
-        pack_w(nc.scalar.copy, 0)
-        pack_x(nc.vector.tensor_copy, 0)
-        pack_x(nc.vector.tensor_copy, 1)
-        quantize_x(0)
-        quantize_x(1)
-        pack_w(nc.vector.tensor_copy, 1)
-        quantize_x(2)
-        quantize_w(0)
-        tap(z_sum, 0)
-        quantize_w(1)
-        tap(z_sum, 1)
-        pack_w(nc.vector.tensor_copy, 2)
-        pack_w(nc.vector.tensor_copy, 3)
-        quantize_w(2)
-        tap(gate_sum, 2)
-        quantize_w(3)
-        tap(gate_sum, 3)
-
-        tanh_z, gate, y, y_round, y_rows, y_packed, y_codes = [], [], [], [], [], [], []
+        tanh_z, gate, y, y_round, y_rows = [], [], [], [], []
         for h, (start, width) in enumerate(PIECES):
             tanh_z.append([sb.tile([P, width], F32, name="tanh%d_%d" % (h, g)) for g in range(G)])
             gate.append([sb.tile([P, width], F32, name="gate%d_%d" % (h, g)) for g in range(G)])
             y.append(sb.tile([P, G, width], F32, name="y%d" % h))
             y_round.append([sb.tile([P, width], BF16, name="y_round%d_%d" % (h, g)) for g in range(G)])
             y_rows.append(sb.tile([P, PACK, width], BF16, name="y_rows%d" % h, align_bytes=64))
-            y_packed.append(sb.tile([P, width, PACK], BF16, name="y_packed%d" % h, align_bytes=64))
-            y_codes.append(sb.tile([P, width], U32, name="y_codes%d" % h, align_bytes=64))
+        y_packed = [sb.tile([P, STEP, PACK], BF16, name="y_packed%d" % k, align_bytes=64) for k in range(N // STEP)]
+        y_codes = sb.tile([P, N], U32, name="y_codes", align_bytes=64)
         y_scales = sb.tile([P, N], U8, name="y_scales", align_bytes=64)
 
         def columns(h):
@@ -140,41 +136,81 @@ def tile_rows_pl_conv_wave_kernel(tc, x, w0, w1, u0, u1, out_0, out_1, out_2):
         def do_gate(h, g):
             nc.scalar.activation(out=gate[h][g][:], in_=gate_sum[g][:, columns(h)], func=ACT.Sigmoid)
 
-        for g in range(G):
+        pack_w(nc.vector.tensor_copy, 0)
+        pack_w(nc.vector.tensor_copy, 1)
+        quantize_w(0)
+        quantize_w(1)
+        pack_x(nc.scalar.copy, 2)
+        pack_w(nc.scalar.copy, 2)
+        pack_w(nc.scalar.copy, 3)
+        pack_x(nc.vector.tensor_copy, 0)
+        pack_x(nc.vector.tensor_copy, 1)
+        quantize_x(0)
+        quantize_x(1)
+        convolve(z_sum, 0, 0)
+        quantize_x(2)
+        convolve(z_sum, 0, 1)
+        quantize_w(2)
+        quantize_w(3)
+        convolve(gate_sum, 2, 0)
+        convolve(gate_sum, 2, 1)
+        for g in ORDER:
             do_tanh(0, g)
-        for g in range(G):
+        for g in ORDER:
             do_gate(0, g)
-        for h in range(1, len(PIECES)):
-            for g in range(G):
-                do_tanh(h, g)
-                do_gate(h, g)
+        pack_x(nc.vector.tensor_copy, 3)
+        pack_x(nc.vector.tensor_copy, 4)
+        quantize_x(3)
+        quantize_x(4)
+        convolve(z_sum, 0, 2)
+        convolve(z_sum, 0, 3)
+        for g in ORDER:
+            convolve(gate_sum, 2, 2, [g])
+            convolve(gate_sum, 2, 3, [g])
+        for g in ORDER:
+            do_tanh(1, g)
+            do_gate(1, g)
 
         y_out = out_0.rearrange("(g m) n -> m g n", g=G)
         words_out = out_1[0].rearrange("p n u -> p (n u)").bitcast(I32)
         scales_out = out_2[0].bitcast(I32)
 
-        def product(h, g):
-            nc.vector.tensor_tensor(out=y[h][:, g, :], in0=tanh_z[h][g][:], in1=gate[h][g][:], op=ALU.mult)
+        def product(h, g, target):
+            nc.vector.tensor_tensor(out=target, in0=tanh_z[h][g][:], in1=gate[h][g][:], op=ALU.mult)
+
+        def regroup(h, g):
+            nc.sync.dma_start(out=y_rows[h][ROWS * g : ROWS * (g + 1), :, :], in_=y_round[h][g][:])
+
+        def store_y(h):
+            nc.sync.dma_start(out=y_out[:, :, columns(h)], in_=y[h][:])
 
         def round_and_regroup(h, g):
             nc.vector.tensor_copy(out=y_round[h][g][:], in_=y[h][:, g, :])
-            nc.sync.dma_start(out=y_rows[h][ROWS * g : ROWS * (g + 1), :, :], in_=y_round[h][g][:])
-            if g == G - 1:
-                nc.sync.dma_start(out=y_out[:, :, columns(h)], in_=y[h][:])
+            regroup(h, g)
 
-        units = [(h, g) for h in range(len(PIECES)) for g in range(G)]
-        for i, (h, g) in enumerate(units):
-            product(h, g)
+        units = [(h, g) for h in range(len(PIECES)) for g in ORDER]
+        for i, (h, g) in enumerate(units[:-1]):
+            product(h, g, y[h][:, g, :])
             if i > 0:
                 round_and_regroup(*units[i - 1])
-        round_and_regroup(*units[-1])
+            if i == G:
+                store_y(0)
+        round_and_regroup(*units[-2])
+        h, g = units[-1]
+        product(h, g, y_round[h][g][:])
+        regroup(h, g)
+        product(h, g, y[h][:, g, :])
+        store_y(1)
 
         for h in range(len(PIECES)):
-            interleave(nc.vector.tensor_copy, y_packed[h][:], y_rows[h][:])
-            quantize(nc, y_codes[h][:], y_scales[:, columns(h)], y_packed[h][:])
-            nc.sync.dma_start(out=words_out[:, columns(h)], in_=y_codes[h][:].bitcast(I32))
+            for k in range(2):
+                interleave(nc.vector.tensor_copy, y_packed[2 * h + k][:], y_rows[h][:, :, k * STEP : (k + 1) * STEP])
+            for k in range(2):
+                cols = slice((2 * h + k) * STEP, (2 * h + k + 1) * STEP)
+                quantize(nc, y_codes[:, cols], y_scales[:, cols], y_packed[2 * h + k][:])
+            nc.sync.dma_start(out=words_out[:, columns(h)], in_=y_codes[:, columns(h)].bitcast(I32))
         for q in range(4):
-            queue = nc.sync if q < 2 else nc.scalar
+            queue = nc.sync if q < 1 else nc.scalar
             queue.dma_start(
                 out=scales_out[4 * q : 4 * q + 4, :],
                 in_=y_scales[32 * q : 32 * q + 4, :].bitcast(I32),

@@ -60,9 +60,9 @@ def tile_rows_pl_conv_wave_kernel(tc, x, w0, w1, u0, u1, out_0, out_1, out_2):
         def load_w(k):
             nc.sync.dma_start(out=w_raw[k][:], in_=weights[k].rearrange("g (p j) m -> (g p) j m", j=PACK))
 
+        load_x(0)
         load_w(0)
         load_w(1)
-        load_x(0)
         load_w(2)
         load_w(3)
         load_x(1)
@@ -136,20 +136,20 @@ def tile_rows_pl_conv_wave_kernel(tc, x, w0, w1, u0, u1, out_0, out_1, out_2):
         def do_gate(h, g):
             nc.scalar.activation(out=gate[h][g][:], in_=gate_sum[g][:, columns(h)], func=ACT.Sigmoid)
 
-        pack_w(nc.vector.tensor_copy, 0)
-        pack_w(nc.vector.tensor_copy, 1)
-        quantize_w(0)
-        quantize_w(1)
         pack_x(nc.scalar.copy, 2)
+        pack_w(nc.scalar.copy, 0)
         pack_w(nc.scalar.copy, 2)
-        pack_w(nc.scalar.copy, 3)
         pack_x(nc.vector.tensor_copy, 0)
         pack_x(nc.vector.tensor_copy, 1)
         quantize_x(0)
         quantize_x(1)
-        convolve(z_sum, 0, 0)
         quantize_x(2)
+        pack_w(nc.vector.tensor_copy, 1)
+        quantize_w(0)
+        quantize_w(1)
+        convolve(z_sum, 0, 0)
         convolve(z_sum, 0, 1)
+        pack_w(nc.vector.tensor_copy, 3)
         quantize_w(2)
         quantize_w(3)
         convolve(gate_sum, 2, 0)
@@ -167,9 +167,6 @@ def tile_rows_pl_conv_wave_kernel(tc, x, w0, w1, u0, u1, out_0, out_1, out_2):
         for g in ORDER:
             convolve(gate_sum, 2, 2, [g])
             convolve(gate_sum, 2, 3, [g])
-        for g in ORDER:
-            do_tanh(1, g)
-            do_gate(1, g)
 
         y_out = out_0.rearrange("(g m) n -> m g n", g=G)
         words_out = out_1[0].rearrange("p n u -> p (n u)").bitcast(I32)
@@ -182,24 +179,35 @@ def tile_rows_pl_conv_wave_kernel(tc, x, w0, w1, u0, u1, out_0, out_1, out_2):
             nc.sync.dma_start(out=y_rows[h][ROWS * g : ROWS * (g + 1), :, :], in_=y_round[h][g][:])
 
         def store_y(h):
-            nc.sync.dma_start(out=y_out[:, :, columns(h)], in_=y[h][:])
+            nc.scalar.dma_start(out=y_out[:, :, columns(h)], in_=y[h][:])
 
         def round_and_regroup(h, g):
             nc.vector.tensor_copy(out=y_round[h][g][:], in_=y[h][:, g, :])
             regroup(h, g)
 
-        units = [(h, g) for h in range(len(PIECES)) for g in ORDER]
-        for i, (h, g) in enumerate(units[:-1]):
-            product(h, g, y[h][:, g, :])
-            if i > 0:
-                round_and_regroup(*units[i - 1])
-            if i == G:
+        def activations(h, g):
+            do_tanh(h, g)
+            do_gate(h, g)
+
+        previous = None
+        for g in ORDER:
+            product(0, g, y[0][:, g, :])
+            if previous is not None:
+                round_and_regroup(*previous)
+            previous = (0, g)
+        for i, g in enumerate(ORDER[:-1]):
+            activations(1, g)
+            product(1, g, y[1][:, g, :])
+            round_and_regroup(*previous)
+            if i == 1:
                 store_y(0)
-        round_and_regroup(*units[-2])
-        h, g = units[-1]
-        product(h, g, y_round[h][g][:])
-        regroup(h, g)
-        product(h, g, y[h][:, g, :])
+            previous = (1, g)
+        g = ORDER[-1]
+        activations(1, g)
+        round_and_regroup(*previous)
+        product(1, g, y_round[1][g][:])
+        regroup(1, g)
+        product(1, g, y[1][:, g, :])
         store_y(1)
 
         for h in range(len(PIECES)):
@@ -210,7 +218,7 @@ def tile_rows_pl_conv_wave_kernel(tc, x, w0, w1, u0, u1, out_0, out_1, out_2):
                 quantize(nc, y_codes[:, cols], y_scales[:, cols], y_packed[2 * h + k][:])
             nc.sync.dma_start(out=words_out[:, columns(h)], in_=y_codes[:, columns(h)].bitcast(I32))
         for q in range(4):
-            queue = nc.sync if q < 1 else nc.scalar
+            queue = nc.sync if q < 2 else nc.scalar
             queue.dma_start(
                 out=scales_out[4 * q : 4 * q + 4, :],
                 in_=y_scales[32 * q : 32 * q + 4, :].bitcast(I32),

from contextlib import ExitStack

import concourse.mybir as mybir

G, D, M, N, DILATION = 4, 128, 128, 512, 128
L = N + DILATION
FLOPS = 2 * 4 * G * D * M * N

F32 = mybir.dt.float32
BF16 = mybir.dt.bfloat16
I32 = mybir.dt.int32
U32 = mybir.dt.uint32
U8 = mybir.dt.uint8
FP8X4 = mybir.dt.float8_e4m3fn_x4
ACT = mybir.ActivationFunctionType
ALU = mybir.AluOpType

P = 128
PACK = 4
ROWS = D // PACK
RUN = 4
STEP = 128
X_LOADS = [(0, 384), (384, 256)]
ORDER = [0, 2, 1, 3]
PIECES = [(0, 256), (256, 256)]


def interleave(copy, packed, raw):
    copy(
        out=packed.rearrange("p (c i) j -> p c j i", i=RUN),
        in_=raw.rearrange("p j (c i) -> p c j i", i=RUN),
    )


def quantize(nc, codes, scales, packed):
    nc.vector.quantize_mx(
        out=codes.bitcast(FP8X4), scales=scales, in_=packed.rearrange("p c j -> p (c j)")
    )


def tile_rows_pl_conv_wave_kernel(tc, x, w0, w1, u0, u1, out_0, out_1, out_2):
    nc = tc.nc
    weights = [w0, w1, u0, u1]
    with ExitStack() as ctx:
        sb = ctx.enter_context(tc.tile_pool(name="sb", bufs=1))
        ps = ctx.enter_context(tc.psum_pool(name="ps", bufs=1))
        ctx.enter_context(tc.manual_schedule())

        x_rows = x.rearrange("g (p j) l -> (g p) j l", j=PACK)
        x_raw = [
            sb.tile([P, PACK, width], F32, name="x_raw%d" % k, align_bytes=64)
            for k, (start, width) in enumerate(X_LOADS)
        ]
        w_raw = [sb.tile([P, PACK, M], F32, name="w_raw%d" % k, align_bytes=64) for k in range(4)]

        def load_x(k):
            start, width = X_LOADS[k]
            nc.sync.dma_start(out=x_raw[k][:], in_=x_rows[:, :, start : start + width])

        def load_w(k):
            nc.sync.dma_start(out=w_raw[k][:], in_=weights[k].rearrange("g (p j) m -> (g p) j m", j=PACK))

        load_x(0)
        load_w(0)
        load_w(1)
        load_w(2)
        load_w(3)
        load_x(1)

        warm_in = sb.tile([P, 8], F32, name="warm_in")
        warm_out = sb.tile([P, 8], F32, name="warm_out")
        nc.vector.memset(warm_in[:], 0.0)
        nc.scalar.activation(out=warm_out[:], in_=warm_in[:], func=ACT.Sigmoid)

        x_packed = [
            sb.tile([P, STEP, PACK], BF16, name="x_packed%d" % k, align_bytes=64)
            for k in range(L // STEP)
        ]
        x_codes = [sb.tile([P, STEP], U32, name="x_codes%d" % k, align_bytes=64) for k in range(L // STEP)]
        x_scales = [sb.tile([P, STEP], U8, name="x_scales%d" % k, align_bytes=64) for k in range(L // STEP)]
        w_packed = [sb.tile([P, M, PACK], BF16, name="w_packed%d" % k, align_bytes=64) for k in range(4)]
        w_codes = [sb.tile([P, M], U32, name="w_codes%d" % k, align_bytes=64) for k in range(4)]
        w_scales = [sb.tile([P, M], U8, name="w_scales%d" % k, align_bytes=64) for k in range(4)]

        def pack_x(copy, k):
            load = 0 if k * STEP < X_LOADS[1][0] else 1
            first = k * STEP - X_LOADS[load][0]
            interleave(copy, x_packed[k][:], x_raw[load][:, :, first : first + STEP])

        def quantize_x(k):
            quantize(nc, x_codes[k][:], x_scales[k][:], x_packed[k][:])

        def pack_w(copy, k):
            interleave(copy, w_packed[k][:], w_raw[k][:])

        def quantize_w(k):
            quantize(nc, w_codes[k][:], w_scales[k][:], w_packed[k][:])

        z_sum = [ps.tile([P, N], F32, name="z_sum%d" % g) for g in range(G)]
        gate_sum = [ps.tile([P, N], F32, name="gate_sum%d" % g) for g in range(G)]

        def convolve(sums, first_weight, step, groups=ORDER):
            cols = slice(step * STEP, (step + 1) * STEP)
            for t in range(2):
                k = first_weight + t
                for g in groups:
                    rows = slice(ROWS * g, ROWS * (g + 1))
                    nc.tensor.matmul_mx(
                        out=sums[g][:, cols],
                        lhsT=w_codes[k][rows, :].bitcast(FP8X4),
                        lhsT_scale=w_scales[k][rows, :],
                        rhs=x_codes[step + t][rows, :].bitcast(FP8X4),
                        rhs_scale=x_scales[step + t][rows, :],
                        start=(t == 0),
                        stop=(t == 1),
                    )

        tanh_z, gate, y, y_round, y_rows = [], [], [], [], []
        for h, (start, width) in enumerate(PIECES):
            tanh_z.append([sb.tile([P, width], F32, name="tanh%d_%d" % (h, g)) for g in range(G)])
            gate.append([sb.tile([P, width], F32, name="gate%d_%d" % (h, g)) for g in range(G)])
            y.append(sb.tile([P, G, width], F32, name="y%d" % h))
            y_round.append([sb.tile([P, width], BF16, name="y_round%d_%d" % (h, g)) for g in range(G)])
            y_rows.append(sb.tile([P, PACK, width], BF16, name="y_rows%d" % h, align_bytes=64))
        y_packed = [sb.tile([P, STEP, PACK], BF16, name="y_packed%d" % k, align_bytes=64) for k in range(N // STEP)]
        y_codes = sb.tile([P, N], U32, name="y_codes", align_bytes=64)
        y_scales = sb.tile([P, N], U8, name="y_scales", align_bytes=64)

        def columns(h):
            start, width = PIECES[h]
            return slice(start, start + width)

        def do_tanh(h, g):
            nc.scalar.activation(out=tanh_z[h][g][:], in_=z_sum[g][:, columns(h)], func=ACT.Tanh)

        def do_gate(h, g):
            nc.scalar.activation(out=gate[h][g][:], in_=gate_sum[g][:, columns(h)], func=ACT.Sigmoid)

        pack_x(nc.scalar.copy, 2)
        pack_w(nc.scalar.copy, 0)
        pack_w(nc.scalar.copy, 2)
        pack_x(nc.vector.tensor_copy, 0)
        pack_x(nc.vector.tensor_copy, 1)
        quantize_x(0)
        quantize_x(1)
        quantize_x(2)
        pack_w(nc.vector.tensor_copy, 1)
        quantize_w(0)
        quantize_w(1)
        convolve(z_sum, 0, 0)
        convolve(z_sum, 0, 1)
        pack_w(nc.vector.tensor_copy, 3)
        quantize_w(2)
        quantize_w(3)
        convolve(gate_sum, 2, 0)
        convolve(gate_sum, 2, 1)
        for g in ORDER:
            do_tanh(0, g)
        for g in ORDER:
            do_gate(0, g)
        pack_x(nc.vector.tensor_copy, 3)
        pack_x(nc.vector.tensor_copy, 4)
        quantize_x(3)
        quantize_x(4)
        convolve(z_sum, 0, 2)
        convolve(z_sum, 0, 3)
        for g in ORDER:
            convolve(gate_sum, 2, 2, [g])
            convolve(gate_sum, 2, 3, [g])

        y_out = out_0.rearrange("(g m) n -> m g n", g=G)
        words_out = out_1[0].rearrange("p n u -> p (n u)").bitcast(I32)
        scales_out = out_2[0].bitcast(I32)

        def product(h, g, target):
            nc.vector.tensor_tensor(out=target, in0=tanh_z[h][g][:], in1=gate[h][g][:], op=ALU.mult)

        def regroup(h, g):
            nc.sync.dma_start(out=y_rows[h][ROWS * g : ROWS * (g + 1), :, :], in_=y_round[h][g][:])

        def store_y(h):
            nc.scalar.dma_start(out=y_out[:, :, columns(h)], in_=y[h][:])

        def round_and_regroup(h, g):
            nc.vector.tensor_copy(out=y_round[h][g][:], in_=y[h][:, g, :])
            regroup(h, g)

        def activations(h, g):
            do_tanh(h, g)
            do_gate(h, g)

        previous = None
        for g in ORDER:
            product(0, g, y[0][:, g, :])
            if previous is not None:
                round_and_regroup(*previous)
            previous = (0, g)
        for i, g in enumerate(ORDER[:-1]):
            activations(1, g)
            product(1, g, y[1][:, g, :])
            round_and_regroup(*previous)
            if i == 1:
                store_y(0)
            previous = (1, g)
        g = ORDER[-1]
        activations(1, g)
        round_and_regroup(*previous)
        product(1, g, y_round[1][g][:])
        regroup(1, g)
        product(1, g, y[1][:, g, :])
        store_y(1)

        for h in range(len(PIECES)):
            for k in range(2):
                interleave(nc.vector.tensor_copy, y_packed[2 * h + k][:], y_rows[h][:, :, k * STEP : (k + 1) * STEP])
            for k in range(2):
                cols = slice((2 * h + k) * STEP, (2 * h + k + 1) * STEP)
                quantize(nc, y_codes[:, cols], y_scales[:, cols], y_packed[2 * h + k][:])
            nc.sync.dma_start(out=words_out[:, columns(h)], in_=y_codes[:, columns(h)].bitcast(I32))
        for q in range(4):
            queue = nc.sync if q < 2 else nc.scalar
            queue.dma_start(
                out=scales_out[4 * q : 4 * q + 4, :],
                in_=y_scales[32 * q : 32 * q + 4, :].bitcast(I32),
            )
